import numpy as np
import ml_dtypes


def mxq(x, axis, fmt="e4m3"):
    dtype, down = {"e4m3": (ml_dtypes.float8_e4m3fn, 7), "e5m2": (ml_dtypes.float8_e5m2, 14)}[fmt]
    v = np.moveaxis(np.asarray(x, np.float32).astype(ml_dtypes.bfloat16).astype(np.float64), axis, -1)
    blocks = v.reshape(v.shape[:-1] + (-1, 32))
    amax = np.abs(blocks).max(-1, keepdims=True)
    byte = np.maximum(np.where(amax > 0, np.frexp(amax)[1] - 1 + 127, 0) - down, 1)
    scale = np.exp2(byte - 127.0)
    codes = (blocks / scale).astype(np.float32).astype(dtype).astype(np.float64)
    return np.moveaxis((codes * scale).reshape(v.shape), -1, axis)


WIDE = False


def mx_kscale(k):
    if not WIDE:
        return np.ones(k)
    levels = np.array([10, -10, 5, -5, 0])
    if k % 512:
        return np.exp2(np.random.permutation(np.resize(levels, k // 32))).repeat(32)
    a = np.empty((k // 512, 16))
    for p in range(k // 512):
        a[p, :8] = np.random.permutation(np.resize(levels, 8))
        for g in range(8):
            far = levels[np.abs(levels - a[p, g]) >= 10]
            a[p, g + 8] = far[np.random.randint(len(far))]
    return np.exp2(a.ravel()).repeat(32)


def f64(x):
    return np.asarray(x).astype(np.float64)


def striped(idx):
    return np.tile(idx.reshape(-1, 16).T, (8, 1)).astype(np.uint16)


def unstriped(offs):
    return offs[:16].T.reshape(-1).astype(np.int64)


E2M1 = np.array([0.0, 0.5, 1.0, 1.5, 2.0, 3.0, 4.0, 6.0, -0.0, -0.5, -1.0, -1.5, -2.0, -3.0, -4.0, -6.0])


def pack_weight(w, fmt):
    k, n = w.shape
    w = f64(np.asarray(w, np.float32).astype(ml_dtypes.bfloat16)).reshape(k // 32, 32, n)
    amax = np.abs(w).max(1)
    if fmt == "e4m3":
        byte = np.frexp(amax)[1] - 1 + 127 - 7
    else:
        mant, ex = np.frexp(amax / 6.0)
        byte = np.where(mant > 0.5, ex, ex - 1) + 127
    byte = np.clip(np.where(amax > 0, byte, 1), 1, 254)
    scaled = (w * np.exp2(127.0 - byte)[:, None, :]).reshape(k, n).astype(np.float32)
    by_word = np.ascontiguousarray(scaled.reshape(k // 512, 128, 4, n).transpose(0, 1, 3, 2))
    if fmt == "e4m3":
        words = by_word.astype(ml_dtypes.float8_e4m3fn).view(np.uint8)
    else:
        c = by_word.astype(ml_dtypes.float4_e2m1fn).view(np.uint8) & 0xF
        words = (c[..., 0::2] | (c[..., 1::2] << 4)).reshape(k // 512, 128, 2 * n)
    return np.ascontiguousarray(words), np.ascontiguousarray(byte.astype(np.uint8).reshape(k // 512, 16, n))


def unpack_weight(words, scales, fmt):
    g, _, n = scales.shape
    words = np.ascontiguousarray(words).reshape(g, 128, n, -1)
    if fmt == "e4m3":
        vals = words.view(ml_dtypes.float8_e4m3fn).astype(np.float64)
    else:
        nib = np.empty((g, 128, n, 4), np.uint8)
        nib[..., 0::2] = words & 0xF
        nib[..., 1::2] = words >> 4
        vals = E2M1[nib]
    vals = vals * np.repeat(np.exp2(scales.astype(np.float64) - 127.0), 8, axis=1)[..., None]
    return vals.transpose(0, 1, 3, 2).reshape(g * 512, n)


G, K, M, T, S = 3, 512, 512, 4096, 512


def setup_inputs():
    n = np.random.standard_normal
    s = mx_kscale(K)[:, None]
    p_w4 = pack_weight(n((K, M)) / np.sqrt(K) / s, "e2m1")
    p_w8 = pack_weight(n((K, M)) / np.sqrt(K) / s, "e4m3")
    return {
        "xT": (n((K, T)) * s).astype(np.float32),
        "c": (n((K, S)) * s).astype(np.float32),
        "w4_words": p_w4[0],
        "w4_scales": p_w4[1],
        "w8_words": p_w8[0],
        "w8_scales": p_w8[1],
        "offs": striped(np.concatenate([np.random.permutation(T)[:S] for _ in range(G)])),
    }


def reference(xT, c, w4_words, w4_scales, w8_words, w8_scales, offs):
    idx = unstriped(offs).reshape(G, S)
    d_ = [mxq(f64(xT)[:, idx[g]] - f64(c), 0, "e4m3") for g in range(G)]
    c_ = mxq(f64(c), 0, "e4m3")
    w4_ = unpack_weight(w4_words, w4_scales, "e2m1")
    w8_ = unpack_weight(w8_words, w8_scales, "e4m3")
    y = np.max([(w4_.T @ d) for d in d_], axis=0) + (w8_.T @ c_)
    return y

@@ -1,0 +1,158 @@
+from contextlib import ExitStack
+
+import concourse.mybir as mybir
+
+G, K, M, T, S = 3, 512, 512, 4096, 512
+FLOPS = 2 * K * M * S * (G + 1)
+
+F32 = mybir.dt.float32
+BF16 = mybir.dt.bfloat16
+I32 = mybir.dt.int32
+U32 = mybir.dt.uint32
+U16 = mybir.dt.uint16
+U8 = mybir.dt.uint8
+FP8X4 = mybir.dt.float8_e4m3fn_x4
+FP4X4 = mybir.dt.float4_e2m1fn_x4
+SUB = mybir.AluOpType.subtract
+MAX = mybir.AluOpType.max
+ADD = mybir.AluOpType.add
+
+P = 128
+PACK = 4
+LIST_COLS = S // 16
+TILES = M // P
+POOL_TILES = 2
+
+
+def tile_list_edge_none_kernel(tc, xT, c, w4_words, w4_scales, w8_words, w8_scales, offs, out):
+    nc = tc.nc
+    x_rows = xT.rearrange("(p i) t -> p i t", i=PACK)
+    c_rows = c.rearrange("(p i) j -> p i j", i=PACK)
+
+    with ExitStack() as ctx:
+        keep = ctx.enter_context(tc.tile_pool(name="keep", bufs=1))
+        psum = ctx.enter_context(tc.psum_pool(name="psum", bufs=1))
+
+        offsets = keep.tile([P, G * LIST_COLS], U16, name="offsets")
+        planes = [keep.tile([P, T], F32, name=f"plane{i}") for i in range(PACK)]
+        c_sb = keep.tile([P, PACK, S], F32, name="c_sb")
+        w4 = keep.tile([P, 2 * M], U8, name="w4", align_bytes=64)
+        w8 = keep.tile([P, 4 * M], U8, name="w8", align_bytes=64)
+        w_scale = keep.tile([P, 2, M], U8, name="w_scale", align_bytes=64)
+
+        nc.sync.dma_start(offsets[:], offs)
+        nc.sync.dma_start(out=planes[0][:], in_=x_rows[:, 0, :])
+        nc.sync.dma_start(out=c_sb[:, 0, :], in_=c_rows[:, 0, :])
+        nc.sync.dma_start(out=planes[1][:], in_=x_rows[:, 1, :])
+        nc.sync.dma_start(out=c_sb[:, 1, :], in_=c_rows[:, 1, :])
+        nc.sync.dma_start(out=planes[2][:], in_=x_rows[:, 2, :])
+        nc.sync.dma_start(out=c_sb[:, 2:4, :], in_=c_rows[:, 2:4, :])
+        nc.sync.dma_start(out=planes[3][:], in_=x_rows[:, 3, :])
+        nc.sync.dma_start(out=w4[:].bitcast(I32), in_=w4_words[0].bitcast(I32))
+        nc.sync.dma_start(out=w8[:].bitcast(I32), in_=w8_words[0].rearrange("p n t -> p (n t)").bitcast(I32))
+
+        nc.gpsimd.memset(w_scale[:].rearrange("p a n -> p (a n)").bitcast(U32), 0)
+        for a, scales in enumerate((w4_scales, w8_scales)):
+            for q in range(4):
+                nc.gpsimd.dma_start(
+                    out=w_scale[32 * q : 32 * q + 4, a, :].bitcast(I32),
+                    in_=scales[0, 4 * q : 4 * q + 4, :].bitcast(I32),
+                )
+
+        picked = [keep.tile([P, G, S], F32, name=f"picked{i}") for i in range(PACK)]
+        diff = keep.tile([P, G, PACK, S], BF16, name="diff")
+        grouped = [keep.tile([P, S, PACK], BF16, name=f"grouped{g}", align_bytes=64) for g in range(G + 1)]
+        codes = [keep.tile([P, S], U32, name=f"codes{g}", align_bytes=64) for g in range(G + 1)]
+        scale = [keep.tile([P, S], U8, name=f"scale{g}", align_bytes=64) for g in range(G + 1)]
+        OWN = G
+
+        def gather(i, g0, g1):
+            nc.vector.tensor_copy(
+                picked[i][:, g0:g1, :].rearrange("p g j -> p (g j)"),
+                planes[i][:].indirect(offsets[:, g0 * LIST_COLS : g1 * LIST_COLS]),
+            )
+
+        def subtract(i, g0, g1):
+            own = c_sb[:, i : i + 1, :].to_broadcast([P, g1 - g0, S])
+            nc.vector.tensor_tensor(diff[:, g0:g1, i, :], picked[i][:, g0:g1, :], own, SUB)
+
+        def interleave(g, source, i0):
+            nc.scalar.copy(
+                out=grouped[g][:, :, i0 : i0 + 2],
+                in_=source[:, i0 : i0 + 2, :].rearrange("p i j -> p j i"),
+            )
+
+        def quantize(g):
+            nc.vector.quantize_mx(
+                out=codes[g][:].bitcast(FP8X4),
+                scales=scale[g][:],
+                in_=grouped[g][:].rearrange("p j i -> p (j i)"),
+            )
+
+        def multiply(g, m, bank):
+            acc = psum.tile([P, S], F32, name=f"acc{g}_{m}", tag=f"bank{bank}")
+            if g == OWN:
+                lhsT = w8[:, 4 * P * m : 4 * P * (m + 1)].bitcast(FP8X4)
+                lhsT_scale = w_scale[:, 1, P * m : P * (m + 1)]
+            else:
+                lhsT = w4[:, 2 * P * m : 2 * P * (m + 1)].bitcast(FP4X4)
+                lhsT_scale = w_scale[:, 0, P * m : P * (m + 1)]
+            nc.tensor.matmul_mx(
+                out=acc[:],
+                lhsT=lhsT,
+                lhsT_scale=lhsT_scale,
+                rhs=codes[g][:].bitcast(FP8X4),
+                rhs_scale=scale[g][:],
+                start=True,
+                stop=True,
+            )
+            return acc
+
+        for i in range(PACK - 1):
+            gather(i, 0, 2)
+            gather(i, 2, 3)
+            subtract(i, 0, 2)
+            subtract(i, 2, 3)
+            if i == 1:
+                interleave(OWN, c_sb, 0)
+                for g in range(G):
+                    interleave(g, diff[:, g], 0)
+        interleave(OWN, c_sb, 2)
+
+        last = PACK - 1
+        best = [keep.tile([P, S], F32, name=f"best{m}") for m in range(TILES)]
+        own_sb = [keep.tile([P, S], F32, name=f"own{m}") for m in range(POOL_TILES)]
+        result = [keep.tile([P, S], F32, name=f"result{m}") for m in range(TILES)]
+
+        for g in range(2):
+            gather(last, g, g + 1)
+            subtract(last, g, g + 1)
+            interleave(g, diff[:, g], 2)
+        quantize(0)
+        acc0 = [multiply(0, m, m) for m in range(TILES)]
+        gather(last, 2, 3)
+        subtract(last, 2, 3)
+        quantize(1)
+        acc1 = [multiply(1, m, TILES + m) for m in range(TILES)]
+        interleave(2, diff[:, 2], 2)
+        for m in range(TILES):
+            nc.scalar.copy(out=best[m][:], in_=acc0[m][:])
+        quantize(OWN)
+        quantize(2)
+        for m in range(TILES):
+            nc.vector.tensor_tensor(best[m][:], acc1[m][:], best[m][:], MAX)
+        acc2 = []
+        acc_own = []
+        for m in range(TILES):
+            acc_own.append(multiply(OWN, m, TILES + m))
+            acc2.append(multiply(2, m, m))
+        for m in range(POOL_TILES):
+            nc.scalar.copy(out=own_sb[m][:], in_=acc_own[m][:])
+        for m in range(TILES):
+            nc.vector.tensor_tensor(best[m][:], acc2[m][:], best[m][:], MAX)
+            if m < POOL_TILES:
+                nc.gpsimd.tensor_tensor(result[m][:], best[m][:], own_sb[m][:], ADD)
+        for m in range(POOL_TILES, TILES):
+            nc.vector.tensor_tensor(result[m][:], acc_own[m][:], best[m][:], ADD)
+        for m in range(TILES):
+            nc.sync.dma_start(out=out[P * m : P * (m + 1), :], in_=result[m][:])

@@ -42,11 +42,9 @@ def tile_list_edge_none_kernel(tc, xT, c, w4_words, w4_scales, w8_words, w8_scal
 
         nc.sync.dma_start(offsets[:], offs)
         nc.sync.dma_start(out=planes[0][:], in_=x_rows[:, 0, :])
-        nc.sync.dma_start(out=c_sb[:, 0, :], in_=c_rows[:, 0, :])
+        nc.sync.dma_start(out=c_sb[:], in_=c_rows)
         nc.sync.dma_start(out=planes[1][:], in_=x_rows[:, 1, :])
-        nc.sync.dma_start(out=c_sb[:, 1, :], in_=c_rows[:, 1, :])
         nc.sync.dma_start(out=planes[2][:], in_=x_rows[:, 2, :])
-        nc.sync.dma_start(out=c_sb[:, 2:4, :], in_=c_rows[:, 2:4, :])
         nc.sync.dma_start(out=planes[3][:], in_=x_rows[:, 3, :])
         nc.sync.dma_start(out=w4[:].bitcast(I32), in_=w4_words[0].bitcast(I32))
         nc.sync.dma_start(out=w8[:].bitcast(I32), in_=w8_words[0].rearrange("p n t -> p (n t)").bitcast(I32))
@@ -60,7 +58,7 @@ def tile_list_edge_none_kernel(tc, xT, c, w4_words, w4_scales, w8_words, w8_scal
                 )
 
         picked = [keep.tile([P, G, S], F32, name=f"picked{i}") for i in range(PACK)]
-        diff = keep.tile([P, G, PACK, S], BF16, name="diff")
+        pairs = [keep.tile([P, 2, S, 2], BF16, name=f"pairs{g}") for g in range(G)]
         grouped = [keep.tile([P, S, PACK], BF16, name=f"grouped{g}", align_bytes=64) for g in range(G + 1)]
         codes = [keep.tile([P, S], U32, name=f"codes{g}", align_bytes=64) for g in range(G + 1)]
         scale = [keep.tile([P, S], U8, name=f"scale{g}", align_bytes=64) for g in range(G + 1)]
@@ -72,14 +70,14 @@ def tile_list_edge_none_kernel(tc, xT, c, w4_words, w4_scales, w8_words, w8_scal
                 planes[i][:].indirect(offsets[:, g0 * LIST_COLS : g1 * LIST_COLS]),
             )
 
-        def subtract(i, g0, g1):
-            own = c_sb[:, i : i + 1, :].to_broadcast([P, g1 - g0, S])
-            nc.vector.tensor_tensor(diff[:, g0:g1, i, :], picked[i][:, g0:g1, :], own, SUB)
+        def subtract(i, g):
+            nc.gpsimd.tensor_tensor(pairs[g][:, i // 2, :, i % 2], picked[i][:, g, :], c_sb[:, i, :], SUB)
 
-        def interleave(g, source, i0):
+        def interleave(g):
+            words = pairs[g][:].rearrange("p u j e -> p (u j e)").bitcast(F32)
             nc.scalar.copy(
-                out=grouped[g][:, :, i0 : i0 + 2],
-                in_=source[:, i0 : i0 + 2, :].rearrange("p i j -> p j i"),
+                out=grouped[g][:].rearrange("p j i -> p (j i)").bitcast(F32).rearrange("p (j u) -> p j u", u=2),
+                in_=words.rearrange("p (u j) -> p j u", u=2),
             )
 
         def quantize(g):
@@ -108,44 +106,38 @@ def tile_list_edge_none_kernel(tc, xT, c, w4_words, w4_scales, w8_words, w8_scal
             )
             return acc
 
+        nc.scalar.copy(out=grouped[OWN][:], in_=c_sb[:].rearrange("p i j -> p j i"))
         for i in range(PACK - 1):
             gather(i, 0, 2)
             gather(i, 2, 3)
-            subtract(i, 0, 2)
-            subtract(i, 2, 3)
-            if i == 1:
-                interleave(OWN, c_sb, 0)
-                for g in range(G):
-                    interleave(g, diff[:, g], 0)
-        interleave(OWN, c_sb, 2)
+            if i == 0:
+                quantize(OWN)
+            for g in range(G):
+                subtract(i, g)
 
         last = PACK - 1
         best = [keep.tile([P, S], F32, name=f"best{m}") for m in range(TILES)]
         own_sb = [keep.tile([P, S], F32, name=f"own{m}") for m in range(POOL_TILES)]
         result = [keep.tile([P, S], F32, name=f"result{m}") for m in range(TILES)]
 
-        for g in range(2):
+        for g in range(G):
             gather(last, g, g + 1)
-            subtract(last, g, g + 1)
-            interleave(g, diff[:, g], 2)
+            subtract(last, g)
+        interleave(0)
+        interleave(1)
         quantize(0)
         acc0 = [multiply(0, m, m) for m in range(TILES)]
-        gather(last, 2, 3)
-        subtract(last, 2, 3)
         quantize(1)
         acc1 = [multiply(1, m, TILES + m) for m in range(TILES)]
-        interleave(2, diff[:, 2], 2)
+        interleave(2)
         for m in range(TILES):
             nc.scalar.copy(out=best[m][:], in_=acc0[m][:])
-        quantize(OWN)
+        acc_own = [multiply(OWN, m, m) for m in range(POOL_TILES)]
         quantize(2)
         for m in range(TILES):
             nc.vector.tensor_tensor(best[m][:], acc1[m][:], best[m][:], MAX)
-        acc2 = []
-        acc_own = []
-        for m in range(TILES):
-            acc_own.append(multiply(OWN, m, TILES + m))
-            acc2.append(multiply(2, m, m))
+        acc2 = [multiply(2, m, (4, 5, 2, 3)[m]) for m in range(TILES)]
+        acc_own += [multiply(OWN, m, TILES + m) for m in range(POOL_TILES, TILES)]
         for m in range(POOL_TILES):
             nc.scalar.copy(out=own_sb[m][:], in_=acc_own[m][:])
         for m in range(TILES):

@@ -21,7 +21,7 @@ P = 128
 PACK = 4
 LIST_COLS = S // 16
 TILES = M // P
-POOL_TILES = 2
+HELD = (S, S, S // 2, 0)
 
 
 def tile_list_edge_none_kernel(tc, xT, c, w4_words, w4_scales, w8_words, w8_scales, offs, out):
@@ -42,10 +42,11 @@ def tile_list_edge_none_kernel(tc, xT, c, w4_words, w4_scales, w8_words, w8_scal
 
         nc.sync.dma_start(offsets[:], offs)
         nc.sync.dma_start(out=planes[0][:], in_=x_rows[:, 0, :])
-        nc.sync.dma_start(out=c_sb[:], in_=c_rows)
+        nc.sync.dma_start(out=c_sb[:, 0:3, :], in_=c_rows[:, 0:3, :])
         nc.sync.dma_start(out=planes[1][:], in_=x_rows[:, 1, :])
         nc.sync.dma_start(out=planes[2][:], in_=x_rows[:, 2, :])
         nc.sync.dma_start(out=planes[3][:], in_=x_rows[:, 3, :])
+        nc.sync.dma_start(out=c_sb[:, 3, :], in_=c_rows[:, 3, :])
         nc.sync.dma_start(out=w4[:].bitcast(I32), in_=w4_words[0].bitcast(I32))
         nc.sync.dma_start(out=w8[:].bitcast(I32), in_=w8_words[0].rearrange("p n t -> p (n t)").bitcast(I32))
 
@@ -57,28 +58,28 @@ def tile_list_edge_none_kernel(tc, xT, c, w4_words, w4_scales, w8_words, w8_scal
                     in_=scales[0, 4 * q : 4 * q + 4, :].bitcast(I32),
                 )
 
-        picked = [keep.tile([P, G, S], F32, name=f"picked{i}") for i in range(PACK)]
-        pairs = [keep.tile([P, 2, S, 2], BF16, name=f"pairs{g}") for g in range(G)]
+        picked = keep.tile([P, PACK, G, S], F32, name="picked")
+        shared = keep.tile([P, 3, S, 2], BF16, name="shared")
+        pairs1 = keep.tile([P, 2, S, 2], BF16, name="pairs1", align_bytes=64)
+        pairs = [shared[:, 1:3], pairs1[:], shared[:, 0:3:2]]
         grouped = [keep.tile([P, S, PACK], BF16, name=f"grouped{g}", align_bytes=64) for g in range(G + 1)]
-        codes = [keep.tile([P, S], U32, name=f"codes{g}", align_bytes=64) for g in range(G + 1)]
+        codes = [keep.tile([P, S], U32, name=f"codes{g}", align_bytes=64) for g in range(G)]
         scale = [keep.tile([P, S], U8, name=f"scale{g}", align_bytes=64) for g in range(G + 1)]
         OWN = G
 
         def gather(i, g0, g1):
             nc.vector.tensor_copy(
-                picked[i][:, g0:g1, :].rearrange("p g j -> p (g j)"),
+                picked[:, i, g0:g1, :].rearrange("p g j -> p (g j)"),
                 planes[i][:].indirect(offsets[:, g0 * LIST_COLS : g1 * LIST_COLS]),
             )
 
-        def subtract(i, g):
-            nc.gpsimd.tensor_tensor(pairs[g][:, i // 2, :, i % 2], picked[i][:, g, :], c_sb[:, i, :], SUB)
+        def subtract(i, g, j0=0, j1=S):
+            nc.gpsimd.tensor_tensor(pairs[g][:, i // 2, j0:j1, i % 2], picked[:, i, g, j0:j1], c_sb[:, i, j0:j1], SUB)
 
-        def interleave(g):
-            words = pairs[g][:].rearrange("p u j e -> p (u j e)").bitcast(F32)
-            nc.scalar.copy(
-                out=grouped[g][:].rearrange("p j i -> p (j i)").bitcast(F32).rearrange("p (j u) -> p j u", u=2),
-                in_=words.rearrange("p (u j) -> p j u", u=2),
-            )
+        def interleave(g, j0=0, j1=S):
+            words = pairs[g].rearrange("p u j e -> p u (j e)").bitcast(F32).rearrange("p u j -> p j u")
+            placed = grouped[g][:].rearrange("p j i -> p (j i)").bitcast(F32).rearrange("p (j u) -> p j u", u=2)
+            nc.scalar.copy(out=placed[:, j0:j1, :], in_=words[:, j0:j1, :])
 
         def quantize(g):
             nc.vector.quantize_mx(
@@ -106,45 +107,92 @@ def tile_list_edge_none_kernel(tc, xT, c, w4_words, w4_scales, w8_words, w8_scal
             )
             return acc
 
-        nc.scalar.copy(out=grouped[OWN][:], in_=c_sb[:].rearrange("p i j -> p j i"))
-        for i in range(PACK - 1):
+        last = PACK - 1
+        nc.scalar.copy(out=grouped[OWN][:, :, 0:last], in_=c_sb[:, 0:last, :].rearrange("p i j -> p j i"))
+        for i in range(last):
             gather(i, 0, 2)
             gather(i, 2, 3)
-            if i == 0:
-                quantize(OWN)
-            for g in range(G):
+            for g in range(G if i < 2 else G - 1):
                 subtract(i, g)
 
-        last = PACK - 1
-        best = [keep.tile([P, S], F32, name=f"best{m}") for m in range(TILES)]
-        own_sb = [keep.tile([P, S], F32, name=f"own{m}") for m in range(POOL_TILES)]
+        best0 = keep.tile([P, S], F32, name="best0")
+        best = [best0[:]]
+        own_sb = [keep.tile([P, HELD[m]], F32, name=f"own{m}") for m in range(TILES - 1)]
         result = [keep.tile([P, S], F32, name=f"result{m}") for m in range(TILES)]
+        acc = {}
 
+        def hold(m):
+            nc.scalar.copy(out=best[m], in_=acc[0, m][:])
+
+        def larger(g, m):
+            nc.vector.tensor_tensor(best[m], acc[g, m][:], best[m], MAX)
+
+        def add_held(m):
+            cols = slice(0, HELD[m])
+            nc.gpsimd.tensor_tensor(result[m][:, cols], best[m][:, cols], own_sb[m][:], ADD)
+
+        def add_from_bank(m):
+            cols = slice(HELD[m], S)
+            nc.vector.tensor_tensor(result[m][:, cols], acc[OWN, m][:, cols], best[m][:, cols], ADD)
+
+        def store(queue, m):
+            queue.dma_start(out=out[P * m : P * (m + 1), :], in_=result[m][:])
+
+        def own_part(m, bank):
+            acc[OWN, m] = multiply(OWN, m, bank)
+            if HELD[m]:
+                nc.scalar.copy(out=own_sb[m][:], in_=acc[OWN, m][:, 0 : HELD[m]])
+
+        nc.scalar.copy(out=grouped[OWN][:, :, last], in_=c_sb[:, last, :])
         for g in range(G):
             gather(last, g, g + 1)
-            subtract(last, g)
-        interleave(0)
+        for j0 in (0, S // 2):
+            subtract(last, 0, j0, j0 + S // 2)
+            interleave(0, j0, j0 + S // 2)
+        subtract(last, 1)
         interleave(1)
         quantize(0)
-        acc0 = [multiply(0, m, m) for m in range(TILES)]
+        nc.vector.tensor_tensor(
+            pairs[2][:, 1],
+            picked[:, 2:4, 2, :].rearrange("p i j -> p j i"),
+            c_sb[:, 2:4, :].rearrange("p i j -> p j i"),
+            SUB,
+        )
         quantize(1)
-        acc1 = [multiply(1, m, TILES + m) for m in range(TILES)]
+        codes.append(keep.tile([P, S], U32, name="codes_own", tag="pairs1", align_bytes=64))
+        quantize(OWN)
+        for g, m in ((0, 0), (0, 1), (1, 0), (0, 2), (1, 1), (0, 3), (1, 2), (1, 3)):
+            acc[g, m] = multiply(g, m, g * TILES + m)
+        hold(0)
         interleave(2)
-        for m in range(TILES):
-            nc.scalar.copy(out=best[m][:], in_=acc0[m][:])
-        acc_own = [multiply(OWN, m, m) for m in range(POOL_TILES)]
+        later = keep.tile([P, TILES - 1, S], F32, name="later", tag="shared")
+        best.extend([later[:, m, :] for m in range(TILES - 1)])
+        hold(1)
+        own_part(0, 0)
+        larger(1, 0)
         quantize(2)
-        for m in range(TILES):
-            nc.vector.tensor_tensor(best[m][:], acc1[m][:], best[m][:], MAX)
-        acc2 = [multiply(2, m, (4, 5, 2, 3)[m]) for m in range(TILES)]
-        acc_own += [multiply(OWN, m, TILES + m) for m in range(POOL_TILES, TILES)]
-        for m in range(POOL_TILES):
-            nc.scalar.copy(out=own_sb[m][:], in_=acc_own[m][:])
-        for m in range(TILES):
-            nc.vector.tensor_tensor(best[m][:], acc2[m][:], best[m][:], MAX)
-            if m < POOL_TILES:
-                nc.gpsimd.tensor_tensor(result[m][:], best[m][:], own_sb[m][:], ADD)
-        for m in range(POOL_TILES, TILES):
-            nc.vector.tensor_tensor(result[m][:], acc_own[m][:], best[m][:], ADD)
-        for m in range(TILES):
-            nc.sync.dma_start(out=out[P * m : P * (m + 1), :], in_=result[m][:])
+        acc[2, 0] = multiply(2, 0, 4)
+        larger(1, 1)
+        hold(2)
+        own_part(1, 1)
+        larger(2, 0)
+        add_held(0)
+        store(nc.sync, 0)
+        acc[2, 1] = multiply(2, 1, 0)
+        hold(3)
+        larger(1, 2)
+        acc[2, 2] = multiply(2, 2, 5)
+        own_part(2, 2)
+        larger(2, 1)
+        add_held(1)
+        store(nc.sync, 1)
+        acc[2, 3] = multiply(2, 3, 4)
+        own_part(3, 3)
+        larger(1, 3)
+        larger(2, 2)
+        add_held(2)
+        larger(2, 3)
+        add_from_bank(2)
+        store(nc.scalar, 2)
+        add_from_bank(3)
+        store(nc.sync, 3)

@@ -40,8 +40,8 @@ def tile_list_edge_none_kernel(tc, xT, c, w4_words, w4_scales, w8_words, w8_scal
         w8 = keep.tile([P, 4 * M], U8, name="w8", align_bytes=64)
         w_scale = keep.tile([P, 2, M], U8, name="w_scale", align_bytes=64)
 
-        nc.sync.dma_start(offsets[:], offs)
         nc.sync.dma_start(out=planes[0][:], in_=x_rows[:, 0, :])
+        nc.sync.dma_start(offsets[:], offs)
         nc.sync.dma_start(out=c_sb[:, 0:3, :], in_=c_rows[:, 0:3, :])
         nc.sync.dma_start(out=planes[1][:], in_=x_rows[:, 1, :])
         nc.sync.dma_start(out=planes[2][:], in_=x_rows[:, 2, :])
@@ -165,12 +165,14 @@ def tile_list_edge_none_kernel(tc, xT, c, w4_words, w4_scales, w8_words, w8_scal
             acc[g, m] = multiply(g, m, g * TILES + m)
         hold(0)
         interleave(2)
-        later = keep.tile([P, TILES - 1, S], F32, name="later", tag="shared")
-        best.extend([later[:, m, :] for m in range(TILES - 1)])
+        best1 = keep.tile([P, S], F32, name="best1", tag="shared")
+        best.append(best1[:])
         hold(1)
         own_part(0, 0)
         larger(1, 0)
         quantize(2)
+        later = keep.tile([P, 2, S], F32, name="later", tag="grouped2", align_bytes=64)
+        best.extend([later[:, 0, :], later[:, 1, :]])
         acc[2, 0] = multiply(2, 0, 4)
         larger(1, 1)
         hold(2)
@@ -191,8 +193,12 @@ def tile_list_edge_none_kernel(tc, xT, c, w4_words, w4_scales, w8_words, w8_scal
         larger(1, 3)
         larger(2, 2)
         add_held(2)
-        larger(2, 3)
+        nc.scalar.dma_start(out=out[2 * P : 3 * P, 0 : S // 2], in_=result[2][:, 0 : S // 2])
+        halves = (slice(0, S // 2), slice(S // 2, S))
+        for cols in halves:
+            nc.vector.tensor_tensor(best[3][:, cols], acc[2, 3][:, cols], best[3][:, cols], MAX)
         add_from_bank(2)
-        store(nc.scalar, 2)
-        add_from_bank(3)
-        store(nc.sync, 3)
+        nc.sync.dma_start(out=out[2 * P : 3 * P, S // 2 : S], in_=result[2][:, S // 2 : S])
+        for cols in halves:
+            nc.vector.tensor_tensor(result[3][:, cols], acc[OWN, 3][:, cols], best[3][:, cols], ADD)
+            nc.sync.dma_start(out=out[3 * P : 4 * P, cols], in_=result[3][:, cols])

from contextlib import ExitStack

import concourse.mybir as mybir

G, K, M, T, S = 3, 512, 512, 4096, 512
FLOPS = 2 * K * M * S * (G + 1)

F32 = mybir.dt.float32
BF16 = mybir.dt.bfloat16
I32 = mybir.dt.int32
U32 = mybir.dt.uint32
U16 = mybir.dt.uint16
U8 = mybir.dt.uint8
FP8X4 = mybir.dt.float8_e4m3fn_x4
FP4X4 = mybir.dt.float4_e2m1fn_x4
SUB = mybir.AluOpType.subtract
MAX = mybir.AluOpType.max
ADD = mybir.AluOpType.add

P = 128
PACK = 4
LIST_COLS = S // 16
TILES = M // P
HELD = (S, S, S // 2, 0)


def tile_list_edge_none_kernel(tc, xT, c, w4_words, w4_scales, w8_words, w8_scales, offs, out):
    nc = tc.nc
    x_rows = xT.rearrange("(p i) t -> p i t", i=PACK)
    c_rows = c.rearrange("(p i) j -> p i j", i=PACK)

    with ExitStack() as ctx:
        keep = ctx.enter_context(tc.tile_pool(name="keep", bufs=1))
        psum = ctx.enter_context(tc.psum_pool(name="psum", bufs=1))

        offsets = keep.tile([P, G * LIST_COLS], U16, name="offsets")
        planes = [keep.tile([P, T], F32, name=f"plane{i}") for i in range(PACK)]
        c_sb = keep.tile([P, PACK, S], F32, name="c_sb")
        w4 = keep.tile([P, 2 * M], U8, name="w4", align_bytes=64)
        w8 = keep.tile([P, 4 * M], U8, name="w8", align_bytes=64)
        w_scale = keep.tile([P, 2, M], U8, name="w_scale", align_bytes=64)

        nc.sync.dma_start(out=planes[0][:], in_=x_rows[:, 0, :])
        nc.sync.dma_start(offsets[:], offs)
        nc.sync.dma_start(out=c_sb[:, 0:3, :], in_=c_rows[:, 0:3, :])
        nc.sync.dma_start(out=planes[1][:], in_=x_rows[:, 1, :])
        nc.sync.dma_start(out=planes[2][:], in_=x_rows[:, 2, :])
        nc.sync.dma_start(out=planes[3][:], in_=x_rows[:, 3, :])
        nc.sync.dma_start(out=c_sb[:, 3, :], in_=c_rows[:, 3, :])
        nc.sync.dma_start(out=w4[:].bitcast(I32), in_=w4_words[0].bitcast(I32))
        nc.sync.dma_start(out=w8[:].bitcast(I32), in_=w8_words[0].rearrange("p n t -> p (n t)").bitcast(I32))

        nc.gpsimd.memset(w_scale[:].rearrange("p a n -> p (a n)").bitcast(U32), 0)
        for a, scales in enumerate((w4_scales, w8_scales)):
            for q in range(4):
                nc.gpsimd.dma_start(
                    out=w_scale[32 * q : 32 * q + 4, a, :].bitcast(I32),
                    in_=scales[0, 4 * q : 4 * q + 4, :].bitcast(I32),
                )

        picked = keep.tile([P, PACK, G, S], F32, name="picked")
        shared = keep.tile([P, 3, S, 2], BF16, name="shared")
        pairs1 = keep.tile([P, 2, S, 2], BF16, name="pairs1", align_bytes=64)
        pairs = [shared[:, 1:3], pairs1[:], shared[:, 0:3:2]]
        grouped = [keep.tile([P, S, PACK], BF16, name=f"grouped{g}", align_bytes=64) for g in range(G + 1)]
        codes = [keep.tile([P, S], U32, name=f"codes{g}", align_bytes=64) for g in range(G)]
        scale = [keep.tile([P, S], U8, name=f"scale{g}", align_bytes=64) for g in range(G + 1)]
        OWN = G

        def gather(i, g0, g1):
            nc.vector.tensor_copy(
                picked[:, i, g0:g1, :].rearrange("p g j -> p (g j)"),
                planes[i][:].indirect(offsets[:, g0 * LIST_COLS : g1 * LIST_COLS]),
            )

        def subtract(i, g, j0=0, j1=S):
            nc.gpsimd.tensor_tensor(pairs[g][:, i // 2, j0:j1, i % 2], picked[:, i, g, j0:j1], c_sb[:, i, j0:j1], SUB)

        def interleave(g, j0=0, j1=S):
            words = pairs[g].rearrange("p u j e -> p u (j e)").bitcast(F32).rearrange("p u j -> p j u")
            placed = grouped[g][:].rearrange("p j i -> p (j i)").bitcast(F32).rearrange("p (j u) -> p j u", u=2)
            nc.scalar.copy(out=placed[:, j0:j1, :], in_=words[:, j0:j1, :])

        def quantize(g):
            nc.vector.quantize_mx(
                out=codes[g][:].bitcast(FP8X4),
                scales=scale[g][:],
                in_=grouped[g][:].rearrange("p j i -> p (j i)"),
            )

        def multiply(g, m, bank):
            acc = psum.tile([P, S], F32, name=f"acc{g}_{m}", tag=f"bank{bank}")
            if g == OWN:
                lhsT = w8[:, 4 * P * m : 4 * P * (m + 1)].bitcast(FP8X4)
                lhsT_scale = w_scale[:, 1, P * m : P * (m + 1)]
            else:
                lhsT = w4[:, 2 * P * m : 2 * P * (m + 1)].bitcast(FP4X4)
                lhsT_scale = w_scale[:, 0, P * m : P * (m + 1)]
            nc.tensor.matmul_mx(
                out=acc[:],
                lhsT=lhsT,
                lhsT_scale=lhsT_scale,
                rhs=codes[g][:].bitcast(FP8X4),
                rhs_scale=scale[g][:],
                start=True,
                stop=True,
            )
            return acc

        last = PACK - 1
        nc.scalar.copy(out=grouped[OWN][:, :, 0:last], in_=c_sb[:, 0:last, :].rearrange("p i j -> p j i"))
        for i in range(last):
            gather(i, 0, 2)
            gather(i, 2, 3)
            for g in range(G if i < 2 else G - 1):
                subtract(i, g)

        best0 = keep.tile([P, S], F32, name="best0")
        best = [best0[:]]
        own_sb = [keep.tile([P, HELD[m]], F32, name=f"own{m}") for m in range(TILES - 1)]
        result = [keep.tile([P, S], F32, name=f"result{m}") for m in range(TILES)]
        acc = {}

        def hold(m):
            nc.scalar.copy(out=best[m], in_=acc[0, m][:])

        def larger(g, m):
            nc.vector.tensor_tensor(best[m], acc[g, m][:], best[m], MAX)

        def add_held(m):
            cols = slice(0, HELD[m])
            nc.gpsimd.tensor_tensor(result[m][:, cols], best[m][:, cols], own_sb[m][:], ADD)

        def add_from_bank(m):
            cols = slice(HELD[m], S)
            nc.vector.tensor_tensor(result[m][:, cols], acc[OWN, m][:, cols], best[m][:, cols], ADD)

        def store(queue, m):
            queue.dma_start(out=out[P * m : P * (m + 1), :], in_=result[m][:])

        def own_part(m, bank):
            acc[OWN, m] = multiply(OWN, m, bank)
            if HELD[m]:
                nc.scalar.copy(out=own_sb[m][:], in_=acc[OWN, m][:, 0 : HELD[m]])

        nc.scalar.copy(out=grouped[OWN][:, :, last], in_=c_sb[:, last, :])
        for g in range(G):
            gather(last, g, g + 1)
        for j0 in (0, S // 2):
            subtract(last, 0, j0, j0 + S // 2)
            interleave(0, j0, j0 + S // 2)
        subtract(last, 1)
        interleave(1)
        quantize(0)
        nc.vector.tensor_tensor(
            pairs[2][:, 1],
            picked[:, 2:4, 2, :].rearrange("p i j -> p j i"),
            c_sb[:, 2:4, :].rearrange("p i j -> p j i"),
            SUB,
        )
        quantize(1)
        codes.append(keep.tile([P, S], U32, name="codes_own", tag="pairs1", align_bytes=64))
        quantize(OWN)
        for g, m in ((0, 0), (0, 1), (1, 0), (0, 2), (1, 1), (0, 3), (1, 2), (1, 3)):
            acc[g, m] = multiply(g, m, g * TILES + m)
        hold(0)
        interleave(2)
        best1 = keep.tile([P, S], F32, name="best1", tag="shared")
        best.append(best1[:])
        hold(1)
        own_part(0, 0)
        larger(1, 0)
        quantize(2)
        later = keep.tile([P, 2, S], F32, name="later", tag="grouped2", align_bytes=64)
        best.extend([later[:, 0, :], later[:, 1, :]])
        acc[2, 0] = multiply(2, 0, 4)
        larger(1, 1)
        hold(2)
        own_part(1, 1)
        larger(2, 0)
        add_held(0)
        store(nc.sync, 0)
        acc[2, 1] = multiply(2, 1, 0)
        hold(3)
        larger(1, 2)
        acc[2, 2] = multiply(2, 2, 5)
        own_part(2, 2)
        larger(2, 1)
        add_held(1)
        store(nc.sync, 1)
        acc[2, 3] = multiply(2, 3, 4)
        own_part(3, 3)
        larger(1, 3)
        larger(2, 2)
        add_held(2)
        nc.scalar.dma_start(out=out[2 * P : 3 * P, 0 : S // 2], in_=result[2][:, 0 : S // 2])
        halves = (slice(0, S // 2), slice(S // 2, S))
        for cols in halves:
            nc.vector.tensor_tensor(best[3][:, cols], acc[2, 3][:, cols], best[3][:, cols], MAX)
        add_from_bank(2)
        nc.sync.dma_start(out=out[2 * P : 3 * P, S // 2 : S], in_=result[2][:, S // 2 : S])
        for cols in halves:
            nc.vector.tensor_tensor(result[3][:, cols], acc[OWN, 3][:, cols], best[3][:, cols], ADD)
            nc.sync.dma_start(out=out[3 * P : 4 * P, cols], in_=result[3][:, cols])
